import numpy as np, ml_dtypes
CORES = [242,247,114,119]
N = 4
import mx_ref
NC, G = 128, 4
C = np.float32(0.000771)
A = np.float32(0.021)
BF = ml_dtypes.bfloat16
def cut(t, i, w=512):
    return t[:, w * i:w * i + w]
def tile(rs):
    return np.stack(rs, axis=2).reshape(128, -1).astype(BF)
def layer(w, X):
    out = []
    for i in range(G):
        for t in range(len(X)):
            p = mx_ref.matmul(mx_ref.quantize(cut(w, len(X) * i + t)), X[t])
            z = p if t == 0 else z + p
        out.append(z)
    return out
def silu(z):
    z = z.astype(np.float64); e = np.exp(-np.abs(z))
    return (z * np.where(z >= 0, 1, e) / (1 + e)).astype(np.float32)
def gate(U, V):
    return [(silu(u * A) * v) * C for u, v in zip(U, V)]
def setup_inputs(rng):
    def f(*shape):
        return mx_ref.flush((rng.standard_normal(shape, dtype=np.float32) * np.exp2(rng.integers(-2, 3, shape[:-1] + (1,)))).astype(BF))
    return {"x": f(N, 128, 4 * NC), "u": f(N, 128, G * 512), "v": f(N, 128, G * 512), "w2": f(N, 128, N * 512)}
def setup_inputs_blocks(rng):
    d = setup_inputs(rng)
    for k in ("v", "w2"): d[k] = mx_ref.spread(d[k], rng, 2)
    for k in ("x", "u"): d[k] = mx_ref.spread(d[k], rng, 1)
    return d
def setup_inputs_wide(rng):
    d = setup_inputs(rng)
    for k in ("v", "w2"): d[k] = mx_ref.flush((d[k].astype(np.float32) * np.exp2(rng.integers(-5, 6, (N, 1, 1))).astype(np.float32)).astype(BF))
    return d
def setup_inputs_zeros(rng):
    d = setup_inputs(rng); v = d["x"].reshape(N, 128, -1, 4).copy()
    v[np.broadcast_to((rng.random((N, 1, v.shape[2], 1)) < 0.33), v.shape)] = 0
    d["x"] = v.reshape(d["x"].shape)
    return d
def reference(x, u, v, w2, own=None):
    h = np.zeros((N, 128, 4 * NC), BF)
    for j in range(N):
        X = [mx_ref.quantize(x[j])]
        h[j] = tile(gate(layer(u[j], X), layer(v[j], X)))
    use = h if own is None else own["h"]
    H = [mx_ref.quantize(use[j]) for j in range(N)]
    y = np.zeros((N, 128, NC), np.float32)
    for r in range(N):
        for j in range(N):
            p = mx_ref.matmul(mx_ref.quantize(cut(w2[r], j)), H[j])
            y[r] = p if j == 0 else y[r] + p
    return {"h": h, "y": y}

@@ -1,0 +1,196 @@
+from concourse.bass import DstId, RemoteDMATransfer
+from concourse.mybir import dt, AluOpType, ActivationFunctionType
+
+N = 4
+G = 4
+TW = 512
+NC = 128
+BANK = 512
+A = 0.021
+C = 0.000771
+V_CUT = 3
+
+SCRATCH = {
+    "xb": ("sbuf", [128, TW], "bfloat16"),
+    "ub": ("sbuf", [128, G * TW], "bfloat16"),
+    "vb": ("sbuf", [128, G * TW], "bfloat16"),
+    "wb": ("sbuf", [128, N * TW], "bfloat16"),
+    "hb": ("sbuf", [128, TW], "bfloat16"),
+    "xq": ("sbuf", [128, NC], "float8_e4m3fn_x4"),
+    "xs": ("sbuf", [128, NC], "uint8"),
+    "uq": ("sbuf", [128, G * NC], "float8_e4m3fn_x4"),
+    "us": ("sbuf", [128, G * NC], "uint8"),
+    "vq": ("sbuf", [128, G * NC], "float8_e4m3fn_x4"),
+    "vs": ("sbuf", [128, G * NC], "uint8"),
+    "wq": ("sbuf", [128, N * NC], "float8_e4m3fn_x4"),
+    "ws": ("sbuf", [128, N * NC], "uint8"),
+    "gq": ("sbuf", [128, N * NC], "float8_e4m3fn_x4"),
+    "gs": ("sbuf", [128, N * NC], "uint8"),
+    "sg": ("sbuf", [128, G * NC], "float32"),
+    "tg": ("sbuf", [128, G * NC], "float32"),
+    "yb": ("sbuf", [128, NC], "float32"),
+    "pu": ("psum", [128, G * BANK], "float32"),
+    "pv": ("psum", [128, G * BANK], "float32"),
+}
+
+SEMAPHORES = (
+    ["ld_x", "ld_u", "ld_v0", "ld_v1", "ld_w", "st_h", "st_y", "q_x", "q_w", "q_h", "m_y", "k_y", "sent"]
+    + ["%s%d" % (p, b) for p in ("q_u", "q_v", "m_u", "m_v", "act", "mul", "fin") for b in range(G)]
+    + ["arr%d" % j for j in range(N)]
+)
+
+
+def _engines(mask):
+    return [e for e in range(16) if (mask >> e) & 1]
+
+
+def _mask(engines):
+    return sum(1 << e for e in engines)
+
+
+def _same_chip(topo, a, b):
+    return topo.host(a) == topo.host(b) and topo.chip(a) == topo.chip(b)
+
+
+def _plan(topo, cores, src):
+    far = [d for d in cores if d != src and not _same_chip(topo, src, d)]
+    near = [d for d in cores if d != src and _same_chip(topo, src, d)]
+    leave = 0
+    out_far, out_near = [], []
+    if far:
+        common = topo.mask(src, far[0])
+        for d in far:
+            common &= topo.mask(src, d)
+        leave = common
+        es = _engines(common)
+        share = 1
+        while share * 2 * len(far) <= len(es):
+            share *= 2
+        for i, d in enumerate(far):
+            out_far.append((d, _mask(es[share * i:share * (i + 1)])))
+    if near:
+        common = topo.mask(src, near[0])
+        for d in near:
+            common &= topo.mask(src, d)
+        es = _engines(common & ~leave) or _engines(common)
+        share = 1
+        while share * 2 * len(near) <= len(es):
+            share *= 2
+        for i, d in enumerate(near):
+            out_near.append((d, _mask(es[share * i:share * (i + 1)])))
+    return out_far, out_near
+
+
+def rank_program(g, core, T, topo):
+    r = T.rank_of(core)
+    if r is None:
+        return
+    S = T.sem
+    cores = list(T.cores)
+    Silu, Copy = ActivationFunctionType.Silu, ActivationFunctionType.Copy
+
+    def tl(buf, i, n=1):
+        return buf[:, TW * i:TW * (i + n)]
+
+    def cw(buf, i):
+        return buf[:, NC * i:NC * (i + 1)]
+
+    def bank(buf, i):
+        return buf[:, BANK * i:BANK * i + NC]
+
+    g.sync.dma_start(T.xb[:], T.x[:]).then_inc(S.ld_x, 16)
+    g.scalar.dma_start(T.ub[:], T.u[:]).then_inc(S.ld_u, 16)
+    g.sync.dma_start(tl(T.vb, 0, V_CUT), tl(T.v, 0, V_CUT)).then_inc(S.ld_v0, 16)
+    g.sync.dma_start(tl(T.vb, V_CUT, G - V_CUT), tl(T.v, V_CUT, G - V_CUT)).then_inc(S.ld_v1, 16)
+    g.sync.dma_start(T.wb[:], T.w2[:]).then_inc(S.ld_w, 16)
+
+    ve = g.vector
+
+    def q_v(b):
+        ve.quantize_mx(cw(T.vq, b), cw(T.vs, b), tl(T.vb, b)).then_inc(S["q_v%d" % b], 1)
+
+    def mul(b):
+        ve.wait_ge(S["act%d" % b], 1)
+        ve.wait_ge(S["m_v%d" % b], 1)
+        ve.tensor_tensor(cw(T.tg, b), cw(T.sg, b), bank(T.pv, b), AluOpType.mult).then_inc(S["mul%d" % b], 1)
+
+    ve.wait_ge(S.ld_x, 16)
+    ve.quantize_mx(T.xq[:], T.xs[:], T.xb[:]).then_inc(S.q_x, 1)
+    ve.wait_ge(S.ld_u, 16)
+    for b in range(G):
+        ve.quantize_mx(cw(T.uq, b), cw(T.us, b), tl(T.ub, b)).then_inc(S["q_u%d" % b], 1)
+    ve.wait_ge(S.ld_v0, 16)
+    for b in range(V_CUT):
+        q_v(b)
+    for b in range(V_CUT - 1):
+        mul(b)
+    ve.wait_ge(S.ld_v1, 16)
+    for b in range(V_CUT, G):
+        q_v(b)
+    for b in range(V_CUT - 1, G):
+        mul(b)
+    for b in range(G):
+        ve.wait_ge(S["fin%d" % b], 1)
+    ve.quantize_mx(cw(T.gq, r), cw(T.gs, r), T.hb[:]).then_inc(S.q_h, 1)
+    ve.wait_ge(S.ld_w, 16)
+    ve.quantize_mx(T.wq[:], T.ws[:], T.wb[:]).then_inc(S.q_w, 1)
+    ve.wait_ge(S.m_y, 1)
+    ve.tensor_copy(T.yb[:], bank(T.pu, 0)).then_inc(S.k_y, 1)
+
+    sc = g.scalar
+    for b in range(G):
+        sc.wait_ge(S["m_u%d" % b], 1)
+        sc.activation(cw(T.sg, b), bank(T.pu, b), Silu, scale=A).then_inc(S["act%d" % b], 1)
+    for b in range(G):
+        sc.wait_ge(S["mul%d" % b], 1)
+        sc.activation(T.hb[:, b:TW:G], cw(T.tg, b), Copy, scale=C).then_inc(S["fin%d" % b], 1)
+
+    far, near = _plan(topo, cores, core)
+    mine = S["arr%d" % r]
+    codes = cw(T.gq, r).bitcast(dt.uint8)
+    plane = cw(T.gs, r)
+    left = 0
+    g.wait_ge(S.q_h, 1)
+    for group in (far, near):
+        if not group:
+            continue
+        for piece in (codes, plane):
+            trs = []
+            for d, m in group:
+                rid, pid = topo.addr(d, core)
+                trs.append(RemoteDMATransfer(dst_ids=[DstId(rid=rid, pnc=pid)], dma_engine_mask=m, remote_sem=mine,
+                                             src=piece, dst=piece))
+                left += len(_engines(m))
+            g.remote_dma_fused(trs, local_sem=S.sent)
+    g.wait_ge(S.sent, left)
+
+    sc.wait_ge(S.sent, left)
+    sc.dma_start(T.h[:], T.hb[:]).then_inc(S.st_h, 16)
+    sc.wait_ge(S.st_h, 16)
+
+    te = g.tensor
+    te.wait_ge(S.q_x, 1)
+    for b in range(G):
+        te.wait_ge(S["q_u%d" % b], 1)
+        te.matmul_mx(bank(T.pu, b), cw(T.uq, b), cw(T.us, b), T.xq[:], T.xs[:], True, True).then_inc(S["m_u%d" % b], 1)
+    for b in range(G):
+        te.wait_ge(S["q_v%d" % b], 1)
+        te.matmul_mx(bank(T.pv, b), cw(T.vq, b), cw(T.vs, b), T.xq[:], T.xs[:], True, True).then_inc(S["m_v%d" % b], 1)
+    order = [core] + [d for d, _m in near] + [d for d, _m in far]
+    te.wait_ge(S.act0, 1)
+    te.wait_ge(S.q_w, 1)
+    for k, src in enumerate(order):
+        j = T.rank_of(src)
+        if src == core:
+            te.wait_ge(S.q_h, 1)
+        else:
+            f, n = _plan(topo, cores, src)
+            m = dict(f + n)[core]
+            te.wait_ge(S["arr%d" % j], 2 * len(_engines(m)))
+        mm = te.matmul_mx(bank(T.pu, 0), cw(T.wq, j), cw(T.ws, j), cw(T.gq, j), cw(T.gs, j), k == 0, k == N - 1)
+        if k == N - 1:
+            mm.then_inc(S.m_y, 1)
+
+    g.sync.wait_ge(S.k_y, 1)
+    g.sync.dma_start(T.y[:], T.yb[:]).then_inc(S.st_y, 16)
+    g.sync.wait_ge(S.st_y, 16)

@@ -8,7 +8,6 @@ NC = 128
 BANK = 512
 A = 0.021
 C = 0.000771
-V_CUT = 3
 
 SCRATCH = {
     "xb": ("sbuf", [128, TW], "bfloat16"),
@@ -34,8 +33,8 @@ SCRATCH = {
 }
 
 SEMAPHORES = (
-    ["ld_x", "ld_u", "ld_v0", "ld_v1", "ld_w", "st_h", "st_y", "q_x", "q_w", "q_h", "m_y", "k_y", "sent"]
-    + ["%s%d" % (p, b) for p in ("q_u", "q_v", "m_u", "m_v", "act", "mul", "fin") for b in range(G)]
+    ["ld_x", "ld_u", "ld_v", "ld_w", "st_h", "st_y", "q_x", "q_h", "m_y", "k_y", "sent0", "sent"]
+    + ["%s%d" % (p, b) for p in ("q_u", "q_v", "q_w", "m_u", "m_v", "act", "mul", "fin") for b in range(G)]
     + ["arr%d" % j for j in range(N)]
 )
 
@@ -88,56 +87,48 @@ def rank_program(g, core, T, topo):
     S = T.sem
     cores = list(T.cores)
     Silu, Copy = ActivationFunctionType.Silu, ActivationFunctionType.Copy
+    ve, sc, te, sy = g.vector, g.scalar, g.tensor, g.sync
 
     def tl(buf, i, n=1):
         return buf[:, TW * i:TW * (i + n)]
 
-    def cw(buf, i):
-        return buf[:, NC * i:NC * (i + 1)]
+    def cw(buf, i, n=1):
+        return buf[:, NC * i:NC * (i + n)]
 
     def bank(buf, i):
         return buf[:, BANK * i:BANK * i + NC]
 
-    g.sync.dma_start(T.xb[:], T.x[:]).then_inc(S.ld_x, 16)
-    g.scalar.dma_start(T.ub[:], T.u[:]).then_inc(S.ld_u, 16)
-    g.sync.dma_start(tl(T.vb, 0, V_CUT), tl(T.v, 0, V_CUT)).then_inc(S.ld_v0, 16)
-    g.sync.dma_start(tl(T.vb, V_CUT, G - V_CUT), tl(T.v, V_CUT, G - V_CUT)).then_inc(S.ld_v1, 16)
-    g.sync.dma_start(T.wb[:], T.w2[:]).then_inc(S.ld_w, 16)
+    far, near = _plan(topo, cores, core)
+    order = [core] + [d for d, _m in near] + [d for d, _m in far]
 
-    ve = g.vector
-
-    def q_v(b):
-        ve.quantize_mx(cw(T.vq, b), cw(T.vs, b), tl(T.vb, b)).then_inc(S["q_v%d" % b], 1)
-
-    def mul(b):
-        ve.wait_ge(S["act%d" % b], 1)
-        ve.wait_ge(S["m_v%d" % b], 1)
-        ve.tensor_tensor(cw(T.tg, b), cw(T.sg, b), bank(T.pv, b), AluOpType.mult).then_inc(S["mul%d" % b], 1)
+    sy.dma_start(T.xb[:], T.x[:]).then_inc(S.ld_x, 16)
+    sc.dma_start(T.ub[:], T.u[:]).then_inc(S.ld_u, 16)
+    sy.dma_start(T.vb[:], T.v[:]).then_inc(S.ld_v, 16)
+    sc.wait_ge(S.ld_x, 16)
+    sc.dma_start(T.wb[:], T.w2[:]).then_inc(S.ld_w, 16)
 
     ve.wait_ge(S.ld_x, 16)
     ve.quantize_mx(T.xq[:], T.xs[:], T.xb[:]).then_inc(S.q_x, 1)
     ve.wait_ge(S.ld_u, 16)
     for b in range(G):
         ve.quantize_mx(cw(T.uq, b), cw(T.us, b), tl(T.ub, b)).then_inc(S["q_u%d" % b], 1)
-    ve.wait_ge(S.ld_v0, 16)
-    for b in range(V_CUT):
-        q_v(b)
-    for b in range(V_CUT - 1):
-        mul(b)
-    ve.wait_ge(S.ld_v1, 16)
-    for b in range(V_CUT, G):
-        q_v(b)
-    for b in range(V_CUT - 1, G):
-        mul(b)
+    ve.wait_ge(S.ld_v, 16)
+    for b in range(G):
+        ve.quantize_mx(cw(T.vq, b), cw(T.vs, b), tl(T.vb, b)).then_inc(S["q_v%d" % b], 1)
+    for b in range(G):
+        ve.wait_ge(S["act%d" % b], 1)
+        ve.wait_ge(S["m_v%d" % b], 1)
+        ve.tensor_tensor(cw(T.tg, b), cw(T.sg, b), bank(T.pv, b), AluOpType.mult).then_inc(S["mul%d" % b], 1)
     for b in range(G):
         ve.wait_ge(S["fin%d" % b], 1)
     ve.quantize_mx(cw(T.gq, r), cw(T.gs, r), T.hb[:]).then_inc(S.q_h, 1)
     ve.wait_ge(S.ld_w, 16)
-    ve.quantize_mx(T.wq[:], T.ws[:], T.wb[:]).then_inc(S.q_w, 1)
+    for src in order:
+        j = T.rank_of(src)
+        ve.quantize_mx(cw(T.wq, j), cw(T.ws, j), tl(T.wb, j)).then_inc(S["q_w%d" % j], 1)
     ve.wait_ge(S.m_y, 1)
     ve.tensor_copy(T.yb[:], bank(T.pu, 0)).then_inc(S.k_y, 1)
 
-    sc = g.scalar
     for b in range(G):
         sc.wait_ge(S["m_u%d" % b], 1)
         sc.activation(cw(T.sg, b), bank(T.pu, b), Silu, scale=A).then_inc(S["act%d" % b], 1)
@@ -145,11 +136,11 @@ def rank_program(g, core, T, topo):
         sc.wait_ge(S["mul%d" % b], 1)
         sc.activation(T.hb[:, b:TW:G], cw(T.tg, b), Copy, scale=C).then_inc(S["fin%d" % b], 1)
 
-    far, near = _plan(topo, cores, core)
     mine = S["arr%d" % r]
     codes = cw(T.gq, r).bitcast(dt.uint8)
     plane = cw(T.gs, r)
-    left = 0
+    left = [0, 0]
+    calls = 0
     g.wait_ge(S.q_h, 1)
     for group in (far, near):
         if not group:
@@ -160,15 +151,16 @@ def rank_program(g, core, T, topo):
                 rid, pid = topo.addr(d, core)
                 trs.append(RemoteDMATransfer(dst_ids=[DstId(rid=rid, pnc=pid)], dma_engine_mask=m, remote_sem=mine,
                                              src=piece, dst=piece))
-                left += len(_engines(m))
-            g.remote_dma_fused(trs, local_sem=S.sent)
-    g.wait_ge(S.sent, left)
+                left[min(calls, 1)] += len(_engines(m))
+            g.remote_dma_fused(trs, local_sem=S.sent if calls else S.sent0)
+            calls += 1
+    g.wait_ge(S.sent0, left[0])
+    g.wait_ge(S.sent, left[1])
 
-    sc.wait_ge(S.sent, left)
+    sc.wait_ge(S.sent0, left[0])
     sc.dma_start(T.h[:], T.hb[:]).then_inc(S.st_h, 16)
     sc.wait_ge(S.st_h, 16)
 
-    te = g.tensor
     te.wait_ge(S.q_x, 1)
     for b in range(G):
         te.wait_ge(S["q_u%d" % b], 1)
@@ -176,9 +168,7 @@ def rank_program(g, core, T, topo):
     for b in range(G):
         te.wait_ge(S["q_v%d" % b], 1)
         te.matmul_mx(bank(T.pv, b), cw(T.vq, b), cw(T.vs, b), T.xq[:], T.xs[:], True, True).then_inc(S["m_v%d" % b], 1)
-    order = [core] + [d for d, _m in near] + [d for d, _m in far]
     te.wait_ge(S.act0, 1)
-    te.wait_ge(S.q_w, 1)
     for k, src in enumerate(order):
         j = T.rank_of(src)
         if src == core:
@@ -187,10 +177,11 @@ def rank_program(g, core, T, topo):
             f, n = _plan(topo, cores, src)
             m = dict(f + n)[core]
             te.wait_ge(S["arr%d" % j], 2 * len(_engines(m)))
+        te.wait_ge(S["q_w%d" % j], 1)
         mm = te.matmul_mx(bank(T.pu, 0), cw(T.wq, j), cw(T.ws, j), cw(T.gq, j), cw(T.gs, j), k == 0, k == N - 1)
         if k == N - 1:
             mm.then_inc(S.m_y, 1)
 
-    g.sync.wait_ge(S.k_y, 1)
-    g.sync.dma_start(T.y[:], T.yb[:]).then_inc(S.st_y, 16)
-    g.sync.wait_ge(S.st_y, 16)
+    sy.wait_ge(S.k_y, 1)
+    sy.dma_start(T.y[:], T.yb[:]).then_inc(S.st_y, 16)
+    sy.wait_ge(S.st_y, 16)

from concourse.bass import DstId, RemoteDMATransfer
from concourse.mybir import dt, AluOpType, ActivationFunctionType

N = 4
G = 4
TW = 512
NC = 128
BANK = 512
A = 0.021
C = 0.000771

SCRATCH = {
    "xb": ("sbuf", [128, TW], "bfloat16"),
    "ub": ("sbuf", [128, G * TW], "bfloat16"),
    "vb": ("sbuf", [128, G * TW], "bfloat16"),
    "wb": ("sbuf", [128, N * TW], "bfloat16"),
    "hb": ("sbuf", [128, TW], "bfloat16"),
    "xq": ("sbuf", [128, NC], "float8_e4m3fn_x4"),
    "xs": ("sbuf", [128, NC], "uint8"),
    "uq": ("sbuf", [128, G * NC], "float8_e4m3fn_x4"),
    "us": ("sbuf", [128, G * NC], "uint8"),
    "vq": ("sbuf", [128, G * NC], "float8_e4m3fn_x4"),
    "vs": ("sbuf", [128, G * NC], "uint8"),
    "wq": ("sbuf", [128, N * NC], "float8_e4m3fn_x4"),
    "ws": ("sbuf", [128, N * NC], "uint8"),
    "gq": ("sbuf", [128, N * NC], "float8_e4m3fn_x4"),
    "gs": ("sbuf", [128, N * NC], "uint8"),
    "sg": ("sbuf", [128, G * NC], "float32"),
    "tg": ("sbuf", [128, G * NC], "float32"),
    "yb": ("sbuf", [128, NC], "float32"),
    "pu": ("psum", [128, G * BANK], "float32"),
    "pv": ("psum", [128, G * BANK], "float32"),
}

SEMAPHORES = (
    ["ld_x", "ld_u", "ld_v", "ld_w", "st_h", "st_y", "q_x", "q_h", "m_y", "k_y", "sent0", "sent"]
    + ["%s%d" % (p, b) for p in ("q_u", "q_v", "q_w", "m_u", "m_v", "act", "mul", "fin") for b in range(G)]
    + ["arr%d" % j for j in range(N)]
)


def _engines(mask):
    return [e for e in range(16) if (mask >> e) & 1]


def _mask(engines):
    return sum(1 << e for e in engines)


def _same_chip(topo, a, b):
    return topo.host(a) == topo.host(b) and topo.chip(a) == topo.chip(b)


def _plan(topo, cores, src):
    far = [d for d in cores if d != src and not _same_chip(topo, src, d)]
    near = [d for d in cores if d != src and _same_chip(topo, src, d)]
    leave = 0
    out_far, out_near = [], []
    if far:
        common = topo.mask(src, far[0])
        for d in far:
            common &= topo.mask(src, d)
        leave = common
        es = _engines(common)
        share = 1
        while share * 2 * len(far) <= len(es):
            share *= 2
        for i, d in enumerate(far):
            out_far.append((d, _mask(es[share * i:share * (i + 1)])))
    if near:
        common = topo.mask(src, near[0])
        for d in near:
            common &= topo.mask(src, d)
        es = _engines(common & ~leave) or _engines(common)
        share = 1
        while share * 2 * len(near) <= len(es):
            share *= 2
        for i, d in enumerate(near):
            out_near.append((d, _mask(es[share * i:share * (i + 1)])))
    return out_far, out_near


def rank_program(g, core, T, topo):
    r = T.rank_of(core)
    if r is None:
        return
    S = T.sem
    cores = list(T.cores)
    Silu, Copy = ActivationFunctionType.Silu, ActivationFunctionType.Copy
    ve, sc, te, sy = g.vector, g.scalar, g.tensor, g.sync

    def tl(buf, i, n=1):
        return buf[:, TW * i:TW * (i + n)]

    def cw(buf, i, n=1):
        return buf[:, NC * i:NC * (i + n)]

    def bank(buf, i):
        return buf[:, BANK * i:BANK * i + NC]

    far, near = _plan(topo, cores, core)
    order = [core] + [d for d, _m in near] + [d for d, _m in far]

    sy.dma_start(T.xb[:], T.x[:]).then_inc(S.ld_x, 16)
    sc.dma_start(T.ub[:], T.u[:]).then_inc(S.ld_u, 16)
    sy.dma_start(T.vb[:], T.v[:]).then_inc(S.ld_v, 16)
    sc.wait_ge(S.ld_x, 16)
    sc.dma_start(T.wb[:], T.w2[:]).then_inc(S.ld_w, 16)

    ve.wait_ge(S.ld_x, 16)
    ve.quantize_mx(T.xq[:], T.xs[:], T.xb[:]).then_inc(S.q_x, 1)
    ve.wait_ge(S.ld_u, 16)
    for b in range(G):
        ve.quantize_mx(cw(T.uq, b), cw(T.us, b), tl(T.ub, b)).then_inc(S["q_u%d" % b], 1)
    ve.wait_ge(S.ld_v, 16)
    for b in range(G):
        ve.quantize_mx(cw(T.vq, b), cw(T.vs, b), tl(T.vb, b)).then_inc(S["q_v%d" % b], 1)
    for b in range(G):
        ve.wait_ge(S["act%d" % b], 1)
        ve.wait_ge(S["m_v%d" % b], 1)
        ve.tensor_tensor(cw(T.tg, b), cw(T.sg, b), bank(T.pv, b), AluOpType.mult).then_inc(S["mul%d" % b], 1)
    for b in range(G):
        ve.wait_ge(S["fin%d" % b], 1)
    ve.quantize_mx(cw(T.gq, r), cw(T.gs, r), T.hb[:]).then_inc(S.q_h, 1)
    ve.wait_ge(S.ld_w, 16)
    for src in order:
        j = T.rank_of(src)
        ve.quantize_mx(cw(T.wq, j), cw(T.ws, j), tl(T.wb, j)).then_inc(S["q_w%d" % j], 1)
    ve.wait_ge(S.m_y, 1)
    ve.tensor_copy(T.yb[:], bank(T.pu, 0)).then_inc(S.k_y, 1)

    for b in range(G):
        sc.wait_ge(S["m_u%d" % b], 1)
        sc.activation(cw(T.sg, b), bank(T.pu, b), Silu, scale=A).then_inc(S["act%d" % b], 1)
    for b in range(G):
        sc.wait_ge(S["mul%d" % b], 1)
        sc.activation(T.hb[:, b:TW:G], cw(T.tg, b), Copy, scale=C).then_inc(S["fin%d" % b], 1)

    mine = S["arr%d" % r]
    codes = cw(T.gq, r).bitcast(dt.uint8)
    plane = cw(T.gs, r)
    left = [0, 0]
    calls = 0
    g.wait_ge(S.q_h, 1)
    for group in (far, near):
        if not group:
            continue
        for piece in (codes, plane):
            trs = []
            for d, m in group:
                rid, pid = topo.addr(d, core)
                trs.append(RemoteDMATransfer(dst_ids=[DstId(rid=rid, pnc=pid)], dma_engine_mask=m, remote_sem=mine,
                                             src=piece, dst=piece))
                left[min(calls, 1)] += len(_engines(m))
            g.remote_dma_fused(trs, local_sem=S.sent if calls else S.sent0)
            calls += 1
    g.wait_ge(S.sent0, left[0])
    g.wait_ge(S.sent, left[1])

    sc.wait_ge(S.sent0, left[0])
    sc.dma_start(T.h[:], T.hb[:]).then_inc(S.st_h, 16)
    sc.wait_ge(S.st_h, 16)

    te.wait_ge(S.q_x, 1)
    for b in range(G):
        te.wait_ge(S["q_u%d" % b], 1)
        te.matmul_mx(bank(T.pu, b), cw(T.uq, b), cw(T.us, b), T.xq[:], T.xs[:], True, True).then_inc(S["m_u%d" % b], 1)
    for b in range(G):
        te.wait_ge(S["q_v%d" % b], 1)
        te.matmul_mx(bank(T.pv, b), cw(T.vq, b), cw(T.vs, b), T.xq[:], T.xs[:], True, True).then_inc(S["m_v%d" % b], 1)
    te.wait_ge(S.act0, 1)
    for k, src in enumerate(order):
        j = T.rank_of(src)
        if src == core:
            te.wait_ge(S.q_h, 1)
        else:
            f, n = _plan(topo, cores, src)
            m = dict(f + n)[core]
            te.wait_ge(S["arr%d" % j], 2 * len(_engines(m)))
        te.wait_ge(S["q_w%d" % j], 1)
        mm = te.matmul_mx(bank(T.pu, 0), cw(T.wq, j), cw(T.ws, j), cw(T.gq, j), cw(T.gs, j), k == 0, k == N - 1)
        if k == N - 1:
            mm.then_inc(S.m_y, 1)

    sy.wait_ge(S.k_y, 1)
    sy.dma_start(T.y[:], T.yb[:]).then_inc(S.st_y, 16)
    sy.wait_ge(S.st_y, 16)
